import numpy as np
import ml_dtypes


def mxq(x, axis, fmt="e4m3"):
    dtype, down = {"e4m3": (ml_dtypes.float8_e4m3fn, 7), "e5m2": (ml_dtypes.float8_e5m2, 14)}[fmt]
    v = np.moveaxis(np.asarray(x, np.float32).astype(ml_dtypes.bfloat16).astype(np.float64), axis, -1)
    blocks = v.reshape(v.shape[:-1] + (-1, 32))
    amax = np.abs(blocks).max(-1, keepdims=True)
    byte = np.maximum(np.where(amax > 0, np.frexp(amax)[1] - 1 + 127, 0) - down, 1)
    scale = np.exp2(byte - 127.0)
    codes = (blocks / scale).astype(np.float32).astype(dtype).astype(np.float64)
    return np.moveaxis((codes * scale).reshape(v.shape), -1, axis)


WIDE = False


def mx_kscale(k):
    if not WIDE:
        return np.ones(k)
    levels = np.array([10, -10, 5, -5, 0])
    if k % 512:
        return np.exp2(np.random.permutation(np.resize(levels, k // 32))).repeat(32)
    a = np.empty((k // 512, 16))
    for p in range(k // 512):
        a[p, :8] = np.random.permutation(np.resize(levels, 8))
        for g in range(8):
            far = levels[np.abs(levels - a[p, g]) >= 10]
            a[p, g + 8] = far[np.random.randint(len(far))]
    return np.exp2(a.ravel()).repeat(32)


def f64(x):
    return np.asarray(x).astype(np.float64)


def split(x):
    m, e = np.frexp(f64(x))
    hi = np.ldexp(np.trunc(16.0 * m) / 16.0, e)
    return hi, f64(x) - hi


def gelu(v):
    return 0.5 * v * (1.0 + np.tanh(np.sqrt(2.0 / np.pi) * (v + 0.044715 * v**3)))


K, M, T = 512, 1536, 1536


def setup_inputs():
    n = np.random.standard_normal
    s = mx_kscale(K)[:, None]
    return {
        "w": (n((K, M)) / np.sqrt(K) / s).astype(np.float32),
        "x": (n((K, T)) * s).astype(np.float32),
        "b": (0.3 * n(1536)).astype(np.float32),
    }


def reference(w, x, b):
    w_hi, w_lo = split(w)
    w_hi_, w_lo_ = mxq(w_hi, 0, "e4m3"), mxq(w_lo, 0, "e4m3")
    x_ = mxq(f64(x), 0, "e4m3")
    y = x_.T @ w_hi_ + x_.T @ w_lo_
    return gelu(y + f64(b)[None, :])

@@ -1,0 +1,234 @@
+from contextlib import ExitStack
+
+import concourse.mybir as mybir
+from concourse.masks import make_identity
+
+K, N, T = 512, 1536, 1536
+FLOPS = 2 * 2 * K * N * T
+
+F32 = mybir.dt.float32
+BF16 = mybir.dt.bfloat16
+I32 = mybir.dt.int32
+U32 = mybir.dt.uint32
+U8 = mybir.dt.uint8
+FP8X4 = mybir.dt.float8_e4m3fn_x4
+ALU = mybir.AluOpType
+GELU = mybir.ActivationFunctionType.Gelu_apprx_tanh
+
+P = 128
+PACK = 4
+BANK = 512
+MASK = -983056
+
+
+def schedule():
+    s = [("ldw", 0, 128), ("ldb",), ("ldw", 128, 256), ("ldw", 256, 512), ("ldw", 512, 768), ("ldw", 768, 1024), ("ldx", 0, 256), ("ldw", 1024, 1536), ("ldx", 256, 768), ("ldx", 768, 1536)]
+    s += [("bt", 0), ("bt", 1), ("bt", 2)]
+    s += [("u", 0, 64, "V"), ("u", 64, 128, "V"), ("mask", 0, 64), ("mask", 64, 128), ("lo", 0, 64, "V"), ("lo", 64, 128, "V"), ("qhi", 0, 128)]
+    s += [("u", 128, 256, "S"), ("u", 256, 384, "S"), ("u", 384, 512, "S"), ("u", 512, 768, "S"), ("u", 768, 1024, "S"), ("bc", 0, "S"), ("xc", 0, 256, "S"), ("bc", 1, "S")]
+    s += [("mask", 128, 256), ("qlo", 0, 128), ("lo", 128, 256, "V"), ("mask", 256, 384), ("qlo", 128, 256), ("lo", 256, 384, "V")]
+    s += [("mask", 384, 512), ("qhi", 128, 384), ("lo", 384, 512, "V"), ("qhi", 384, 512)]
+    s += [("mask", 512, 768), ("qlo", 256, 512), ("lo", 512, 768, "V"), ("qhi", 512, 768)]
+    s += [("mask", 768, 1024), ("qlo", 512, 768), ("qx", 0, 256), ("mm", 0, 0), ("mm", 1, 0), ("lo", 768, 1024, "V"), ("qhi", 768, 1024)]
+    s += [("u", 1024, 1280, "S"), ("u", 1280, 1536, "S"), ("xc", 256, 512, "S")]
+    s += [("mask", 1024, 1280), ("qlo", 768, 1024), ("mm", 0, 1), ("mm", 1, 1)]
+    s += [("lo", 1024, 1152, "G")]
+    s += [("add", 0, 0, 512), ("gelu", 0, 0, 512), ("st", 0, 0, 512), ("add", 1, 0, 512), ("add", 0, 512, 1024)]
+    s += [("xc", 512, 768, "S"), ("bc", 2, "S")]
+    s += [("qx", 256, 512), ("mm", 2, 0), ("mm", 2, 1), ("mm", 3, 0), ("mm", 3, 1)]
+    s += [("mask", 1280, 1536), ("qhi", 1024, 1280), ("qlo", 1024, 1152), ("lo", 1152, 1280, "G")]
+    s += [("add", 1, 512, 1024), ("gelu", 0, 512, 1024), ("st", 0, 512, 1024), ("gelu", 1, 0, 1024), ("st", 1, 0, 1024)]
+    s += [("add", 2, 0, 512), ("add", 2, 512, 1024), ("gelu", 2, 0, 1024), ("st", 2, 0, 1024)]
+    s += [("qx", 512, 768), ("mm", 4, 0), ("mm", 4, 1), ("mm", 5, 0), ("mm", 5, 1)]
+    s += [("lo", 1408, 1536, "V"), ("qhi", 1280, 1536), ("qlo", 1408, 1536), ("qlo", 1152, 1280), ("lo", 1280, 1408, "G")]
+    s += [("add", 3, 0, 512), ("add", 3, 512, 1024), ("gelu", 3, 0, 1024), ("st", 3, 0, 1024), ("add", 4, 0, 512)]
+    s += [("qlo", 1280, 1408), ("xc", 768, 1024, "G")]
+    s += [("mm", t, 2) for t in range(5)]
+    order = [(4, 1), (5, 0), (5, 1)] + [(t, 2) for t in range(5)]
+    mms = [(5, 2)] + [(t, c) for t in range(6, 12) for c in range(3)]
+    order += mms
+    late = {(0, 2): [("qx", 768, 1024), ("xc", 1024, 1280, "G")], (4, 2): [("qx", 1024, 1280), ("xc", 1280, 1536, "G")], (6, 2): [("qx", 1280, 1536)]}
+    issued = 0
+    for q, (t, c) in enumerate(order):
+        if (t, c) == (11, 2):
+            for h in (1024, 1280):
+                s += [("add", t, h, h + 256), ("gelu", t, h, h + 256), ("st", t, h, h + 256)]
+            break
+        s += [("add", t, c * 512, c * 512 + 512)]
+        s += late.get((t, c), [])
+        while issued <= q and issued < len(mms) and (q >= 3 or issued == 0):
+            s += [("mm",) + mms[issued]]
+            issued += 1
+        if t < 6 and c > 0:
+            a = 0 if c == 1 else 1024
+            s += [("gelu", t, a, c * 512 + 512), ("st", t, a, c * 512 + 512)]
+        elif t >= 11:
+            s += [("gelu", t, c * 512, c * 512 + 512), ("st", t, c * 512, c * 512 + 512)]
+        elif t >= 6 and c == 1:
+            s += [("gelu", t, 0, 1024), ("st", t, 0, 1024)]
+        elif t >= 6 and c == 2:
+            s += [("gelu", t, 1024, 1536), ("st", t, 1024, 1536)]
+    return s
+
+
+def tile_mix_hilo_tm_gelu_kernel(tc, w, x, b, out):
+    nc = tc.nc
+    engines = {"V": nc.vector, "S": nc.scalar, "G": nc.gpsimd}
+
+    with ExitStack() as ctx:
+        keep = ctx.enter_context(tc.tile_pool(name="keep", bufs=1))
+        psum = ctx.enter_context(tc.psum_pool(name="psum", bufs=8))
+
+        hi_bf = keep.tile([P, PACK * N], BF16, align_bytes=64)
+        lo_bf = keep.tile([P, PACK * N], BF16, align_bytes=64)
+        hi_codes = keep.tile([P, N], U32, align_bytes=64)
+        lo_codes = keep.tile([P, N], U32, align_bytes=64)
+        x_codes = keep.tile([P, T], U32, align_bytes=64)
+        hi_scales = keep.tile([P, N], U8, align_bytes=64)
+        lo_scales = keep.tile([P, N], U8, align_bytes=64)
+        x_scales = keep.tile([P, T], U8, align_bytes=64)
+        bias_cols = keep.tile([P, N // BANK, PACK], F32)
+        bias_rows = keep.tile([P, N], F32)
+        identity = keep.tile([P, P], F32)
+        warm_in = keep.tile([P, 8], F32)
+        warm_out = keep.tile([P, 8], F32)
+
+        raw = {"w": [], "x": []}
+        x_bf = {}
+        lo_stage = {}
+        banks = {}
+        res = {}
+
+        def raw_view(name, a, e):
+            for first, last, piece in raw[name]:
+                if first <= a and e <= last:
+                    return piece, a - first, e - first
+            raise ValueError(name)
+
+        def by_fours(rows):
+            return rows.rearrange("p j (c i) -> p c j i", i=4)
+
+        def grouped_by_fours(cols):
+            return cols.rearrange("p (c i j) -> p c j i", i=4, j=PACK)
+
+        def copy_on(eng, dst, src):
+            if eng == "V":
+                nc.vector.tensor_copy(out=grouped_by_fours(dst), in_=by_fours(src))
+            elif eng == "S":
+                nc.scalar.copy(out=grouped_by_fours(dst), in_=by_fours(src))
+            else:
+                nc.gpsimd.tensor_scalar(
+                    out=dst.rearrange("p (n j) -> p n j", j=PACK),
+                    in0=src.rearrange("p j n -> p n j"),
+                    scalar1=1.0, scalar2=0.0, op0=ALU.mult, op1=ALU.add,
+                )
+
+        ctx.enter_context(tc.manual_schedule())
+        nc.scalar.dma_start(out=bias_cols[:], in_=b.rearrange("(g p c) -> p g c", p=P, c=PACK))
+        nc.gpsimd.memset(warm_in[:], 0.0)
+        nc.scalar.activation(out=warm_out[:], in_=warm_in[:], func=GELU)
+        make_identity(nc, identity[:])
+
+        for step in schedule():
+            kind = step[0]
+            if kind == "ldb":
+                continue
+            elif kind == "ldw" or kind == "ldx":
+                name, src = ("w", w) if kind == "ldw" else ("x", x)
+                a, e = step[1], step[2]
+                piece = keep.tile([P, PACK, e - a], F32, name="raw_%s_%d" % (name, a))
+                nc.sync.dma_start(out=piece[:], in_=src[:, a:e].rearrange("(p j) n -> p j n", j=PACK))
+                raw[name].append((a, e, piece))
+            elif kind == "bt":
+                g = step[1]
+                bank = psum.tile([P, BANK], F32, name="bank")
+                for c in range(PACK):
+                    nc.tensor.transpose(
+                        bank[:, c * P : (c + 1) * P],
+                        bias_cols[:, g, c : c + 1].to_broadcast([P, P]),
+                        identity[:],
+                    )
+                banks[("bias", g)] = bank
+            elif kind == "bc":
+                g = step[1]
+                dst = bias_rows[:, g * BANK : (g + 1) * BANK].rearrange("q (p c) -> q p c", c=PACK)
+                src = banks[("bias", g)][:].rearrange("q (c p) -> q p c", c=PACK)
+                if step[2] == "S":
+                    nc.scalar.copy(out=dst, in_=src)
+                else:
+                    nc.vector.tensor_copy(out=dst, in_=src)
+            elif kind == "u":
+                a, e = step[1], step[2]
+                piece, pa, pe = raw_view("w", a, e)
+                halves = piece[:].bitcast(BF16).rearrange("p j (n h) -> p j n h", h=2)
+                copy_on(step[3], hi_bf[:, PACK * a : PACK * e], halves[:, :, pa:pe, 1])
+            elif kind == "mask":
+                a, e = step[1], step[2]
+                pairs = hi_bf[:, PACK * a : PACK * e].bitcast(I32)
+                nc.vector.tensor_scalar(out=pairs, in0=pairs, scalar1=MASK, scalar2=None, op0=ALU.bitwise_and)
+            elif kind == "lo":
+                a, e = step[1], step[2]
+                piece, pa, pe = raw_view("w", a, e)
+                if step[3] == "V":
+                    nc.vector.tensor_tensor(
+                        out=grouped_by_fours(lo_bf[:, PACK * a : PACK * e]),
+                        in0=by_fours(piece[:, :, pa:pe]),
+                        in1=grouped_by_fours(hi_bf[:, PACK * a : PACK * e]),
+                        op=ALU.subtract,
+                    )
+                else:
+                    stage = keep.tile([P, PACK * (e - a)], BF16, name="gpsimd_stage", align_bytes=64)
+                    lo_stage[a] = stage
+                    nc.gpsimd.tensor_tensor(
+                        out=stage[:].rearrange("p (n j) -> p n j", j=PACK),
+                        in0=piece[:, :, pa:pe].rearrange("p j n -> p n j"),
+                        in1=hi_bf[:, PACK * a : PACK * e].rearrange("p (n j) -> p n j", j=PACK),
+                        op=ALU.subtract,
+                    )
+            elif kind == "qhi":
+                a, e = step[1], step[2]
+                nc.vector.quantize_mx(out=hi_codes[:, a:e].bitcast(FP8X4), scales=hi_scales[:, a:e], in_=hi_bf[:, PACK * a : PACK * e])
+            elif kind == "qlo":
+                a, e = step[1], step[2]
+                src = lo_stage[a][:] if a in lo_stage else lo_bf[:, PACK * a : PACK * e]
+                nc.vector.quantize_mx(out=lo_codes[:, a:e].bitcast(FP8X4), scales=lo_scales[:, a:e], in_=src)
+            elif kind == "xc":
+                a, e = step[1], step[2]
+                piece, pa, pe = raw_view("x", a, e)
+                tag = "gpsimd_stage" if step[3] == "G" else "x_bf_%d" % a
+                stage = keep.tile([P, PACK * (e - a)], BF16, name=tag, align_bytes=64)
+                copy_on(step[3], stage[:], piece[:, :, pa:pe])
+                x_bf[a] = stage
+            elif kind == "qx":
+                a, e = step[1], step[2]
+                nc.vector.quantize_mx(out=x_codes[:, a:e].bitcast(FP8X4), scales=x_scales[:, a:e], in_=x_bf[a][:])
+            elif kind == "mm":
+                t, c = step[1], step[2]
+                bank = psum.tile([P, BANK], F32, name="bank")
+                t_cols = slice(t * P, (t + 1) * P)
+                n_cols = slice(c * BANK, (c + 1) * BANK)
+                for codes, scales, first in ((hi_codes, hi_scales, True), (lo_codes, lo_scales, False)):
+                    nc.tensor.matmul_mx(
+                        out=bank[:],
+                        lhsT=x_codes[:, t_cols].bitcast(FP8X4),
+                        lhsT_scale=x_scales[:, t_cols],
+                        rhs=codes[:, n_cols].bitcast(FP8X4),
+                        rhs_scale=scales[:, n_cols],
+                        start=first,
+                        stop=not first,
+                    )
+                banks[(t, c)] = bank
+            elif kind == "add":
+                t, a, e = step[1], step[2], step[3]
+                if t not in res:
+                    res[t] = keep.tile([P, N], F32, name="res_%d" % t)
+                c = a // BANK
+                nc.vector.tensor_tensor(
+                    out=res[t][:, a:e], in0=banks[(t, c)][:, a - c * BANK : e - c * BANK], in1=bias_rows[:, a:e], op=ALU.add
+                )
+            elif kind == "gelu":
+                t, a, e = step[1], step[2], step[3]
+                nc.scalar.activation(out=res[t][:, a:e], in_=res[t][:, a:e], func=GELU)
+            else:
+                t, a, e = step[1], step[2], step[3]
+                nc.sync.dma_start(out=out[t * P : (t + 1) * P, a:e], in_=res[t][:, a:e])

@@ -22,52 +22,40 @@ MASK = -983056
 
 
 def schedule():
-    s = [("ldw", 0, 128), ("ldb",), ("ldw", 128, 256), ("ldw", 256, 512), ("ldw", 512, 768), ("ldw", 768, 1024), ("ldx", 0, 256), ("ldw", 1024, 1536), ("ldx", 256, 768), ("ldx", 768, 1536)]
-    s += [("bt", 0), ("bt", 1), ("bt", 2)]
-    s += [("u", 0, 64, "V"), ("u", 64, 128, "V"), ("mask", 0, 64), ("mask", 64, 128), ("lo", 0, 64, "V"), ("lo", 64, 128, "V"), ("qhi", 0, 128)]
-    s += [("u", 128, 256, "S"), ("u", 256, 384, "S"), ("u", 384, 512, "S"), ("u", 512, 768, "S"), ("u", 768, 1024, "S"), ("bc", 0, "S"), ("xc", 0, 256, "S"), ("bc", 1, "S")]
-    s += [("mask", 128, 256), ("qlo", 0, 128), ("lo", 128, 256, "V"), ("mask", 256, 384), ("qlo", 128, 256), ("lo", 256, 384, "V")]
-    s += [("mask", 384, 512), ("qhi", 128, 384), ("lo", 384, 512, "V"), ("qhi", 384, 512)]
-    s += [("mask", 512, 768), ("qlo", 256, 512), ("lo", 512, 768, "V"), ("qhi", 512, 768)]
-    s += [("mask", 768, 1024), ("qlo", 512, 768), ("qx", 0, 256), ("mm", 0, 0), ("mm", 1, 0), ("lo", 768, 1024, "V"), ("qhi", 768, 1024)]
-    s += [("u", 1024, 1280, "S"), ("u", 1280, 1536, "S"), ("xc", 256, 512, "S")]
-    s += [("mask", 1024, 1280), ("qlo", 768, 1024), ("mm", 0, 1), ("mm", 1, 1)]
-    s += [("lo", 1024, 1152, "G")]
-    s += [("add", 0, 0, 512), ("gelu", 0, 0, 512), ("st", 0, 0, 512), ("add", 1, 0, 512), ("add", 0, 512, 1024)]
-    s += [("xc", 512, 768, "S"), ("bc", 2, "S")]
-    s += [("qx", 256, 512), ("mm", 2, 0), ("mm", 2, 1), ("mm", 3, 0), ("mm", 3, 1)]
-    s += [("mask", 1280, 1536), ("qhi", 1024, 1280), ("qlo", 1024, 1152), ("lo", 1152, 1280, "G")]
-    s += [("add", 1, 512, 1024), ("gelu", 0, 512, 1024), ("st", 0, 512, 1024), ("gelu", 1, 0, 1024), ("st", 1, 0, 1024)]
-    s += [("add", 2, 0, 512), ("add", 2, 512, 1024), ("gelu", 2, 0, 1024), ("st", 2, 0, 1024)]
-    s += [("qx", 512, 768), ("mm", 4, 0), ("mm", 4, 1), ("mm", 5, 0), ("mm", 5, 1)]
-    s += [("lo", 1408, 1536, "V"), ("qhi", 1280, 1536), ("qlo", 1408, 1536), ("qlo", 1152, 1280), ("lo", 1280, 1408, "G")]
-    s += [("add", 3, 0, 512), ("add", 3, 512, 1024), ("gelu", 3, 0, 1024), ("st", 3, 0, 1024), ("add", 4, 0, 512)]
-    s += [("qlo", 1280, 1408), ("xc", 768, 1024, "G")]
-    s += [("mm", t, 2) for t in range(5)]
-    order = [(4, 1), (5, 0), (5, 1)] + [(t, 2) for t in range(5)]
-    mms = [(5, 2)] + [(t, c) for t in range(6, 12) for c in range(3)]
-    order += mms
-    late = {(0, 2): [("qx", 768, 1024), ("xc", 1024, 1280, "G")], (4, 2): [("qx", 1024, 1280), ("xc", 1280, 1536, "G")], (6, 2): [("qx", 1280, 1536)]}
-    issued = 0
+    s = [("ldw", 0, 256), ("ldb",), ("ldw", 256, 384), ("ldw", 384, 512), ("ldw", 512, 768), ("ldw", 768, 1024), ("ldx", 0, 256), ("ldx", 256, 512), ("ldw", 1024, 1536), ("ldx", 512, 768), ("ldx", 768, 1536)]
+    s += [("bt", 0), ("bt", 1)]
+    s += [("u", 128, 256, "V"), ("u", 0, 128, "S"), ("u", 256, 384, "S"), ("u", 384, 512, "S"), ("bc", 0, "S"), ("u", 512, 768, "S")]
+    s += [("u", 768, 1024, "S"), ("xc", 0, 256, "S"), ("bc", 1, "S"), ("xc", 256, 512, "S")]
+    s += [("u", 1024, 1152, "S"), ("u", 1152, 1536, "S"), ("xc", 512, 768, "S")]
+    s += [("mask", 128, 256), ("mask", 0, 128), ("lo", 128, 256, "V"), ("lo", 0, 128, "V")]
+    s += [("mask", 256, 512), ("qhi", 0, 256), ("lo", 256, 384, "V"), ("lo", 384, 512, "V")]
+    s += [("mask", 512, 768), ("qlo", 0, 512), ("lo", 512, 768, "V"), ("qhi", 256, 512)]
+    s += [("mask", 768, 1024), ("qx", 0, 256), ("mm", 0, 0), ("mm", 1, 0), ("qhi", 512, 1024), ("lo", 768, 1024, "V"), ("qx", 256, 512)]
+    s += [("qlo", 512, 1024), ("mask", 1024, 1152), ("lo", 1024, 1152, "G")]
+    order = [(0, 0), (1, 0), (0, 1), (1, 1)] + [(t, c) for t in range(2, 8) for c in range(2)] + [(t, 2) for t in range(8)] + [(t, c) for t in range(8, 12) for c in range(3)]
+    late = {
+        3: [("xc", 768, 1024, "S"), ("mask", 1152, 1536), ("qx", 512, 768), ("qlo", 1024, 1152), ("lo", 1152, 1280, "G"), ("lo", 1408, 1536, "V")],
+        7: [("qx", 768, 1024), ("qlo", 1152, 1280), ("lo", 1280, 1408, "G"), ("qlo", 1408, 1536), ("bt", 2)],
+        11: [("bc", 2, "S"), ("qhi", 1024, 1536), ("qlo", 1280, 1408), ("xc", 1024, 1280, "G")],
+        16: [("qx", 1024, 1280), ("xc", 1280, 1536, "G")],
+        25: [("qx", 1280, 1536)],
+    }
+    ready = {3: 12, 7: 16, 11: 24, 16: 30, 25: 36}
+    issued = 2
+    limit = 8
     for q, (t, c) in enumerate(order):
-        if (t, c) == (11, 2):
-            for h in (1024, 1280):
-                s += [("add", t, h, h + 256), ("gelu", t, h, h + 256), ("st", t, h, h + 256)]
-            break
-        s += [("add", t, c * 512, c * 512 + 512)]
-        s += late.get((t, c), [])
-        while issued <= q and issued < len(mms) and (q >= 3 or issued == 0):
-            s += [("mm",) + mms[issued]]
+        while issued < min(limit, q + (8 if q < 8 else 7 if q < 12 else 8)):
+            s += [("mm",) + order[issued]]
             issued += 1
-        if t < 6 and c > 0:
-            a = 0 if c == 1 else 1024
-            s += [("gelu", t, a, c * 512 + 512), ("st", t, a, c * 512 + 512)]
-        elif t >= 11:
-            s += [("gelu", t, c * 512, c * 512 + 512), ("st", t, c * 512, c * 512 + 512)]
-        elif t >= 6 and c == 1:
-            s += [("gelu", t, 0, 1024), ("st", t, 0, 1024)]
-        elif t >= 6 and c == 2:
-            s += [("gelu", t, 1024, 1536), ("st", t, 1024, 1536)]
+        a, e = c * 512, c * 512 + 512
+        s += [("add", t, a, e)]
+        s += [("gelu", t, a, e)]
+        if t < 8:
+            s += [("st", t, a, e)]
+        else:
+            s += {0: [("st", t, a, e)], 1: [], 2: [("st", t, 512, 1536)]}[c]
+        s += late.get(q, [])
+        limit = ready.get(q, limit)
     return s
 
 
@@ -79,16 +67,16 @@ def tile_mix_hilo_tm_gelu_kernel(tc, w, x, b, out):
         keep = ctx.enter_context(tc.tile_pool(name="keep", bufs=1))
         psum = ctx.enter_context(tc.psum_pool(name="psum", bufs=8))
 
-        hi_bf = keep.tile([P, PACK * N], BF16, align_bytes=64)
-        lo_bf = keep.tile([P, PACK * N], BF16, align_bytes=64)
-        hi_codes = keep.tile([P, N], U32, align_bytes=64)
-        lo_codes = keep.tile([P, N], U32, align_bytes=64)
-        x_codes = keep.tile([P, T], U32, align_bytes=64)
-        hi_scales = keep.tile([P, N], U8, align_bytes=64)
-        lo_scales = keep.tile([P, N], U8, align_bytes=64)
-        x_scales = keep.tile([P, T], U8, align_bytes=64)
+        hi_bf = keep.tile([P, PACK * N], BF16, align_bytes=256)
+        lo_bf = keep.tile([P, PACK * N], BF16, align_bytes=256)
+        hi_codes = keep.tile([P, N], U32, align_bytes=256)
+        lo_codes = keep.tile([P, N], U32, align_bytes=256)
+        x_codes = keep.tile([P, T], U32, align_bytes=256)
+        hi_scales = keep.tile([P, N], U8, align_bytes=256)
+        lo_scales = keep.tile([P, N], U8, align_bytes=256)
+        x_scales = keep.tile([P, T], U8, align_bytes=256)
         bias_cols = keep.tile([P, N // BANK, PACK], F32)
-        bias_rows = keep.tile([P, N], F32)
+        bias_rows = keep.tile([P, N], F32, align_bytes=256)
         identity = keep.tile([P, P], F32)
         warm_in = keep.tile([P, 8], F32)
         warm_out = keep.tile([P, 8], F32)
@@ -136,7 +124,7 @@ def tile_mix_hilo_tm_gelu_kernel(tc, w, x, b, out):
             elif kind == "ldw" or kind == "ldx":
                 name, src = ("w", w) if kind == "ldw" else ("x", x)
                 a, e = step[1], step[2]
-                piece = keep.tile([P, PACK, e - a], F32, name="raw_%s_%d" % (name, a))
+                piece = keep.tile([P, PACK, e - a], F32, name="raw_%s_%d" % (name, a), align_bytes=256)
                 nc.sync.dma_start(out=piece[:], in_=src[:, a:e].rearrange("(p j) n -> p j n", j=PACK))
                 raw[name].append((a, e, piece))
             elif kind == "bt":
@@ -171,13 +159,13 @@ def tile_mix_hilo_tm_gelu_kernel(tc, w, x, b, out):
                 piece, pa, pe = raw_view("w", a, e)
                 if step[3] == "V":
                     nc.vector.tensor_tensor(
-                        out=grouped_by_fours(lo_bf[:, PACK * a : PACK * e]),
-                        in0=by_fours(piece[:, :, pa:pe]),
-                        in1=grouped_by_fours(hi_bf[:, PACK * a : PACK * e]),
+                        out=lo_bf[:, PACK * a : PACK * e].rearrange("p (c i j) -> p c j i", i=2, j=PACK),
+                        in0=piece[:, :, pa:pe].rearrange("p j (c i) -> p c j i", i=2),
+                        in1=hi_bf[:, PACK * a : PACK * e].rearrange("p (c i j) -> p c j i", i=2, j=PACK),
                         op=ALU.subtract,
                     )
                 else:
-                    stage = keep.tile([P, PACK * (e - a)], BF16, name="gpsimd_stage", align_bytes=64)
+                    stage = keep.tile([P, PACK * (e - a)], BF16, name="gpsimd_stage", align_bytes=256)
                     lo_stage[a] = stage
                     nc.gpsimd.tensor_tensor(
                         out=stage[:].rearrange("p (n j) -> p n j", j=PACK),
@@ -196,7 +184,7 @@ def tile_mix_hilo_tm_gelu_kernel(tc, w, x, b, out):
                 a, e = step[1], step[2]
                 piece, pa, pe = raw_view("x", a, e)
                 tag = "gpsimd_stage" if step[3] == "G" else "x_bf_%d" % a
-                stage = keep.tile([P, PACK * (e - a)], BF16, name=tag, align_bytes=64)
+                stage = keep.tile([P, PACK * (e - a)], BF16, name=tag, align_bytes=256)
                 copy_on(step[3], stage[:], piece[:, :, pa:pe])
                 x_bf[a] = stage
             elif kind == "qx":
@@ -221,7 +209,7 @@ def tile_mix_hilo_tm_gelu_kernel(tc, w, x, b, out):
             elif kind == "add":
                 t, a, e = step[1], step[2], step[3]
                 if t not in res:
-                    res[t] = keep.tile([P, N], F32, name="res_%d" % t)
+                    res[t] = keep.tile([P, N], F32, name="res_%d" % t, align_bytes=256)
                 c = a // BANK
                 nc.vector.tensor_tensor(
                     out=res[t][:, a:e], in0=banks[(t, c)][:, a - c * BANK : e - c * BANK], in1=bias_rows[:, a:e], op=ALU.add

@@ -22,34 +22,23 @@ MASK = -983056
 
 
 def schedule():
-    s = [("ldw", 0, 256), ("ldb",), ("ldw", 256, 384), ("ldw", 384, 512), ("ldw", 512, 768), ("ldw", 768, 1024), ("ldx", 0, 256), ("ldx", 256, 512), ("ldw", 1024, 1536), ("ldx", 512, 768), ("ldx", 768, 1536)]
-    s += [("bt", 0), ("bt", 1)]
-    s += [("u", 128, 256, "V"), ("u", 0, 128, "S"), ("u", 256, 384, "S"), ("u", 384, 512, "S"), ("bc", 0, "S"), ("u", 512, 768, "S")]
-    s += [("u", 768, 1024, "S"), ("xc", 0, 256, "S"), ("bc", 1, "S"), ("xc", 256, 512, "S")]
-    s += [("u", 1024, 1152, "S"), ("u", 1152, 1536, "S"), ("xc", 512, 768, "S")]
+    s = [("ldw", 0, 256), ("ldb",), ("ldw", 256, 384), ("ldw", 384, 512), ("ldw", 512, 768), ("ldw", 768, 1024), ("ldx", 0, 256), ("ldx", 256, 512), ("ldw", 1024, 1280), ("ldx", 512, 1024), ("ldw", 1280, 1536), ("ldx", 1024, 1536)]
+    s += [("bt", 0), ("bt", 1), ("bt", 2)]
+    s += [("u", 128, 256, "V"), ("u", 0, 128, "S"), ("u", 256, 384, "S"), ("u", 384, 512, "S"), ("bc", 0, "S"), ("u", 512, 768, "S"), ("u", 768, 1024, "S"), ("xc", 0, 256, "S"), ("xc", 256, 512, "S"), ("u", 1024, 1280, "S"), ("bc", 1, "S"), ("bc", 2, "S"), ("xc", 512, 640, "S"), ("xc", 640, 896, "S"), ("u", 1280, 1536, "S"), ("xc", 896, 1024, "S")]
     s += [("mask", 128, 256), ("mask", 0, 128), ("lo", 128, 256, "V"), ("lo", 0, 128, "V")]
     s += [("mask", 256, 512), ("qhi", 0, 256), ("lo", 256, 384, "V"), ("lo", 384, 512, "V")]
-    s += [("mask", 512, 768), ("qlo", 0, 512), ("lo", 512, 768, "V"), ("qhi", 256, 512)]
-    s += [("mask", 768, 1024), ("qx", 0, 256), ("mm", 0, 0), ("mm", 1, 0), ("qhi", 512, 1024), ("lo", 768, 1024, "V"), ("qx", 256, 512)]
-    s += [("qlo", 512, 1024), ("mask", 1024, 1152), ("lo", 1024, 1152, "G")]
+    s += [("mask", 512, 768), ("qlo", 0, 512), ("qhi", 256, 512), ("lo", 512, 768, "V"), ("mask", 768, 1024), ("qx", 0, 256), ("mm", 0, 0), ("mm", 1, 0), ("lo", 768, 1024, "V"), ("qhi", 512, 1024), ("qlo", 512, 1024), ("mask", 1024, 1152), ("lo", 1024, 1152, "G"), ("qx", 256, 512)]
     order = [(0, 0), (1, 0), (0, 1), (1, 1)] + [(t, c) for t in range(2, 8) for c in range(2)] + [(t, 2) for t in range(8)] + [(t, c) for t in range(8, 12) for c in range(3)]
-    late = {
-        3: [("xc", 768, 1024, "S"), ("mask", 1152, 1536), ("qx", 512, 768), ("qlo", 1024, 1152), ("lo", 1152, 1280, "G"), ("lo", 1408, 1536, "V")],
-        7: [("qx", 768, 1024), ("qlo", 1152, 1280), ("lo", 1280, 1408, "G"), ("qlo", 1408, 1536), ("bt", 2)],
-        11: [("bc", 2, "S"), ("qhi", 1024, 1536), ("qlo", 1280, 1408), ("xc", 1024, 1280, "G")],
-        16: [("qx", 1024, 1280), ("xc", 1280, 1536, "G")],
-        25: [("qx", 1280, 1536)],
-    }
-    ready = {3: 12, 7: 16, 11: 24, 16: 30, 25: 36}
+    late = {2: [("mask", 1152, 1280), ("qlo", 1024, 1152), ("lo", 1152, 1280, "G"), ("qx", 512, 640)], 5: [("mask", 1280, 1536), ("qlo", 1152, 1280), ("lo", 1280, 1408, "G"), ("qx", 640, 896)], 8: [("qx", 896, 1024), ("qlo", 1280, 1408), ("lo", 1408, 1536, "G"), ("qhi", 1280, 1536)], 11: [("qhi", 1024, 1280), ("qlo", 1408, 1536), ("xc", 1024, 1280, "G")], 16: [("qx", 1024, 1280), ("xc", 1280, 1536, "G")], 25: [("qx", 1280, 1536)]}
+    ready = {2: 10, 5: 14, 8: 16, 11: 24, 16: 30, 25: 36}
     issued = 2
     limit = 8
     for q, (t, c) in enumerate(order):
-        while issued < min(limit, q + (8 if q < 8 else 7 if q < 12 else 8)):
+        while issued < min(limit, q + (7 if 99 < q <= 99 else 8)):
             s += [("mm",) + order[issued]]
             issued += 1
         a, e = c * 512, c * 512 + 512
-        s += [("add", t, a, e)]
-        s += [("gelu", t, a, e)]
+        s += [("add", t, a, e), ("gelu", t, a, e)]
         if t < 8:
             s += [("st", t, a, e)]
         else:

@@ -17,195 +17,238 @@ GELU = mybir.ActivationFunctionType.Gelu_apprx_tanh
 
 P = 128
 PACK = 4
-BANK = 512
-MASK = -983056
+CHUNK = 512
+PSUM_BANKS = 8
+ALIGN = 256
+CHUNKS = N // CHUNK
+ROW_TILES = T // P
+HI_MASK = -983056
+EARLY_TILES = 8
+
+LOADS = (
+    ("w", 0, 256), ("w", 256, 384), ("w", 384, 512), ("w", 512, 768), ("w", 768, 1024),
+    ("x", 0, 256), ("x", 256, 512), ("w", 1024, 1280), ("x", 512, 1024), ("w", 1280, 1536),
+    ("x", 1024, 1536),
+)
 
 
-def schedule():
-    s = [("ldw", 0, 256), ("ldb",), ("ldw", 256, 384), ("ldw", 384, 512), ("ldw", 512, 768), ("ldw", 768, 1024), ("ldx", 0, 256), ("ldx", 256, 512), ("ldw", 1024, 1280), ("ldx", 512, 1024), ("ldw", 1280, 1536), ("ldx", 1024, 1536)]
-    s += [("bt", 0), ("bt", 1), ("bt", 2)]
-    s += [("u", 128, 256, "V"), ("u", 0, 128, "S"), ("u", 256, 384, "S"), ("u", 384, 512, "S"), ("bc", 0, "S"), ("u", 512, 768, "S"), ("u", 768, 1024, "S"), ("xc", 0, 256, "S"), ("xc", 256, 512, "S"), ("u", 1024, 1280, "S"), ("bc", 1, "S"), ("bc", 2, "S"), ("xc", 512, 640, "S"), ("xc", 640, 896, "S"), ("u", 1280, 1536, "S"), ("xc", 896, 1024, "S")]
-    s += [("mask", 128, 256), ("mask", 0, 128), ("lo", 128, 256, "V"), ("lo", 0, 128, "V")]
-    s += [("mask", 256, 512), ("qhi", 0, 256), ("lo", 256, 384, "V"), ("lo", 384, 512, "V")]
-    s += [("mask", 512, 768), ("qlo", 0, 512), ("qhi", 256, 512), ("lo", 512, 768, "V"), ("mask", 768, 1024), ("qx", 0, 256), ("mm", 0, 0), ("mm", 1, 0), ("lo", 768, 1024, "V"), ("qhi", 512, 1024), ("qlo", 512, 1024), ("mask", 1024, 1152), ("lo", 1024, 1152, "G"), ("qx", 256, 512)]
-    order = [(0, 0), (1, 0), (0, 1), (1, 1)] + [(t, c) for t in range(2, 8) for c in range(2)] + [(t, 2) for t in range(8)] + [(t, c) for t in range(8, 12) for c in range(3)]
-    late = {2: [("mask", 1152, 1280), ("qlo", 1024, 1152), ("lo", 1152, 1280, "G"), ("qx", 512, 640)], 5: [("mask", 1280, 1536), ("qlo", 1152, 1280), ("lo", 1280, 1408, "G"), ("qx", 640, 896)], 8: [("qx", 896, 1024), ("qlo", 1280, 1408), ("lo", 1408, 1536, "G"), ("qhi", 1280, 1536)], 11: [("qhi", 1024, 1280), ("qlo", 1408, 1536), ("xc", 1024, 1280, "G")], 16: [("qx", 1024, 1280), ("xc", 1280, 1536, "G")], 25: [("qx", 1280, 1536)]}
-    ready = {2: 10, 5: 14, 8: 16, 11: 24, 16: 30, 25: 36}
-    issued = 2
-    limit = 8
-    for q, (t, c) in enumerate(order):
-        while issued < min(limit, q + (7 if 99 < q <= 99 else 8)):
-            s += [("mm",) + order[issued]]
-            issued += 1
-        a, e = c * 512, c * 512 + 512
-        s += [("add", t, a, e), ("gelu", t, a, e)]
-        if t < 8:
-            s += [("st", t, a, e)]
-        else:
-            s += {0: [("st", t, a, e)], 1: [], 2: [("st", t, 512, 1536)]}[c]
-        s += late.get(q, [])
-        limit = ready.get(q, limit)
-    return s
+def bank_order():
+    order = [(tile, chunk) for chunk in range(2) for tile in range(2)]
+    order += [(tile, chunk) for tile in range(2, EARLY_TILES) for chunk in range(2)]
+    order += [(tile, CHUNKS - 1) for tile in range(EARLY_TILES)]
+    order += [(tile, chunk) for tile in range(EARLY_TILES, ROW_TILES) for chunk in range(CHUNKS)]
+    return order
 
 
 def tile_mix_hilo_tm_gelu_kernel(tc, w, x, b, out):
     nc = tc.nc
-    engines = {"V": nc.vector, "S": nc.scalar, "G": nc.gpsimd}
 
     with ExitStack() as ctx:
         keep = ctx.enter_context(tc.tile_pool(name="keep", bufs=1))
-        psum = ctx.enter_context(tc.psum_pool(name="psum", bufs=8))
+        psum = ctx.enter_context(tc.psum_pool(name="psum", bufs=PSUM_BANKS))
 
-        hi_bf = keep.tile([P, PACK * N], BF16, align_bytes=256)
-        lo_bf = keep.tile([P, PACK * N], BF16, align_bytes=256)
-        hi_codes = keep.tile([P, N], U32, align_bytes=256)
-        lo_codes = keep.tile([P, N], U32, align_bytes=256)
-        x_codes = keep.tile([P, T], U32, align_bytes=256)
-        hi_scales = keep.tile([P, N], U8, align_bytes=256)
-        lo_scales = keep.tile([P, N], U8, align_bytes=256)
-        x_scales = keep.tile([P, T], U8, align_bytes=256)
-        bias_cols = keep.tile([P, N // BANK, PACK], F32)
-        bias_rows = keep.tile([P, N], F32, align_bytes=256)
+        hi_bf = keep.tile([P, PACK * N], BF16, align_bytes=ALIGN)
+        lo_bf = keep.tile([P, PACK * (N - CHUNK)], BF16, align_bytes=ALIGN)
+        hi_codes = keep.tile([P, N], U32, align_bytes=ALIGN)
+        lo_codes = keep.tile([P, N], U32, align_bytes=ALIGN)
+        x_codes = keep.tile([P, T], U32, align_bytes=ALIGN)
+        hi_scales = keep.tile([P, N], U8, align_bytes=ALIGN)
+        lo_scales = keep.tile([P, N], U8, align_bytes=ALIGN)
+        x_scales = keep.tile([P, T], U8, align_bytes=ALIGN)
+        bias_cols = keep.tile([P, CHUNKS, PACK], F32)
+        bias_rows = keep.tile([P, N], F32, align_bytes=ALIGN)
         identity = keep.tile([P, P], F32)
         warm_in = keep.tile([P, 8], F32)
         warm_out = keep.tile([P, 8], F32)
 
-        raw = {"w": [], "x": []}
-        x_bf = {}
-        lo_stage = {}
-        banks = {}
-        res = {}
+        mx = {"hi": (hi_codes, hi_scales), "lo": (lo_codes, lo_scales), "x": (x_codes, x_scales)}
+        loaded = {"w": [], "x": []}
+        staged = {}
+        quantised = {"hi": 0, "lo": 0, "x": 0}
+        bias_banks = []
+        sums = []
+        results = {}
+        order = bank_order()
 
-        def raw_view(name, a, e):
-            for first, last, piece in raw[name]:
-                if first <= a and e <= last:
-                    return piece, a - first, e - first
+        def raw(name, first, end):
+            for piece_first, piece_end, piece in loaded[name]:
+                if piece_first <= first and end <= piece_end:
+                    return piece, slice(first - piece_first, end - piece_first)
             raise ValueError(name)
 
-        def by_fours(rows):
-            return rows.rearrange("p j (c i) -> p c j i", i=4)
+        def packed(tile, first, end):
+            return tile[:, PACK * first : PACK * end]
 
-        def grouped_by_fours(cols):
-            return cols.rearrange("p (c i j) -> p c j i", i=4, j=PACK)
+        def by_rows(rows, run):
+            return rows.rearrange("p j (c i) -> p c j i", i=run)
 
-        def copy_on(eng, dst, src):
-            if eng == "V":
-                nc.vector.tensor_copy(out=grouped_by_fours(dst), in_=by_fours(src))
-            elif eng == "S":
-                nc.scalar.copy(out=grouped_by_fours(dst), in_=by_fours(src))
+        def by_words(words, run):
+            return words.rearrange("p (c i j) -> p c j i", i=run, j=PACK)
+
+        def gpsimd_stage(operand, first, end):
+            stage = keep.tile([P, PACK * (end - first)], BF16, name="gpsimd_stage", align_bytes=ALIGN)
+            staged[(operand, first)] = stage
+            return stage[:].rearrange("p (n j) -> p n j", j=PACK)
+
+        def upper_halves(copy, first, end):
+            piece, cols = raw("w", first, end)
+            halves = piece[:].bitcast(BF16).rearrange("p j (n h) -> p j n h", h=2)
+            copy(out=by_words(packed(hi_bf, first, end), 4), in_=by_rows(halves[:, :, cols, 1], 4))
+
+        def mask_hi(first, end):
+            pairs = packed(hi_bf, first, end).bitcast(I32)
+            nc.vector.tensor_scalar(out=pairs, in0=pairs, scalar1=HI_MASK, scalar2=None, op0=ALU.bitwise_and)
+
+        def low_on_vector(first, end):
+            piece, cols = raw("w", first, end)
+            nc.vector.tensor_tensor(
+                out=by_words(packed(lo_bf, first, end), 2),
+                in0=by_rows(piece[:, :, cols], 2),
+                in1=by_words(packed(hi_bf, first, end), 2),
+                op=ALU.subtract,
+            )
+
+        def low_on_gpsimd(first, end):
+            piece, cols = raw("w", first, end)
+            nc.gpsimd.tensor_tensor(
+                out=gpsimd_stage("lo", first, end),
+                in0=piece[:, :, cols].rearrange("p j n -> p n j"),
+                in1=packed(hi_bf, first, end).rearrange("p (n j) -> p n j", j=PACK),
+                op=ALU.subtract,
+            )
+
+        def cast_x_on_scalar(first, end):
+            piece, cols = raw("x", first, end)
+            stage = keep.tile([P, PACK * (end - first)], BF16, name="x_bf_%d" % first, align_bytes=ALIGN)
+            staged[("x", first)] = stage
+            nc.scalar.copy(out=by_words(stage[:], 4), in_=by_rows(piece[:, :, cols], 4))
+
+        def cast_x_on_gpsimd(first, end):
+            piece, cols = raw("x", first, end)
+            nc.gpsimd.tensor_scalar(
+                out=gpsimd_stage("x", first, end),
+                in0=piece[:, :, cols].rearrange("p j n -> p n j"),
+                scalar1=1.0,
+                scalar2=0.0,
+                op0=ALU.mult,
+                op1=ALU.add,
+            )
+
+        def quantize(operand, first, end):
+            if (operand, first) in staged:
+                values = staged[(operand, first)][:]
             else:
-                nc.gpsimd.tensor_scalar(
-                    out=dst.rearrange("p (n j) -> p n j", j=PACK),
-                    in0=src.rearrange("p j n -> p n j"),
-                    scalar1=1.0, scalar2=0.0, op0=ALU.mult, op1=ALU.add,
-                )
+                values = packed({"hi": hi_bf, "lo": lo_bf}[operand], first, end)
+            codes, scales = mx[operand]
+            nc.vector.quantize_mx(out=codes[:, first:end].bitcast(FP8X4), scales=scales[:, first:end], in_=values)
+            quantised[operand] = end
 
-        ctx.enter_context(tc.manual_schedule())
-        nc.scalar.dma_start(out=bias_cols[:], in_=b.rearrange("(g p c) -> p g c", p=P, c=PACK))
-        nc.gpsimd.memset(warm_in[:], 0.0)
-        nc.scalar.activation(out=warm_out[:], in_=warm_in[:], func=GELU)
-        make_identity(nc, identity[:])
+        def spread_bias(chunk):
+            bank = psum.tile([P, CHUNK], F32, name="bank")
+            for c in range(PACK):
+                column = bias_cols[:, chunk, c : c + 1].to_broadcast([P, P])
+                nc.tensor.transpose(bank[:, c * P : (c + 1) * P], column, identity[:])
+            bias_banks.append(bank)
 
-        for step in schedule():
-            kind = step[0]
-            if kind == "ldb":
-                continue
-            elif kind == "ldw" or kind == "ldx":
-                name, src = ("w", w) if kind == "ldw" else ("x", x)
-                a, e = step[1], step[2]
-                piece = keep.tile([P, PACK, e - a], F32, name="raw_%s_%d" % (name, a), align_bytes=256)
-                nc.sync.dma_start(out=piece[:], in_=src[:, a:e].rearrange("(p j) n -> p j n", j=PACK))
-                raw[name].append((a, e, piece))
-            elif kind == "bt":
-                g = step[1]
-                bank = psum.tile([P, BANK], F32, name="bank")
-                for c in range(PACK):
-                    nc.tensor.transpose(
-                        bank[:, c * P : (c + 1) * P],
-                        bias_cols[:, g, c : c + 1].to_broadcast([P, P]),
-                        identity[:],
-                    )
-                banks[("bias", g)] = bank
-            elif kind == "bc":
-                g = step[1]
-                dst = bias_rows[:, g * BANK : (g + 1) * BANK].rearrange("q (p c) -> q p c", c=PACK)
-                src = banks[("bias", g)][:].rearrange("q (c p) -> q p c", c=PACK)
-                if step[2] == "S":
-                    nc.scalar.copy(out=dst, in_=src)
-                else:
-                    nc.vector.tensor_copy(out=dst, in_=src)
-            elif kind == "u":
-                a, e = step[1], step[2]
-                piece, pa, pe = raw_view("w", a, e)
-                halves = piece[:].bitcast(BF16).rearrange("p j (n h) -> p j n h", h=2)
-                copy_on(step[3], hi_bf[:, PACK * a : PACK * e], halves[:, :, pa:pe, 1])
-            elif kind == "mask":
-                a, e = step[1], step[2]
-                pairs = hi_bf[:, PACK * a : PACK * e].bitcast(I32)
-                nc.vector.tensor_scalar(out=pairs, in0=pairs, scalar1=MASK, scalar2=None, op0=ALU.bitwise_and)
-            elif kind == "lo":
-                a, e = step[1], step[2]
-                piece, pa, pe = raw_view("w", a, e)
-                if step[3] == "V":
-                    nc.vector.tensor_tensor(
-                        out=lo_bf[:, PACK * a : PACK * e].rearrange("p (c i j) -> p c j i", i=2, j=PACK),
-                        in0=piece[:, :, pa:pe].rearrange("p j (c i) -> p c j i", i=2),
-                        in1=hi_bf[:, PACK * a : PACK * e].rearrange("p (c i j) -> p c j i", i=2, j=PACK),
-                        op=ALU.subtract,
-                    )
-                else:
-                    stage = keep.tile([P, PACK * (e - a)], BF16, name="gpsimd_stage", align_bytes=256)
-                    lo_stage[a] = stage
-                    nc.gpsimd.tensor_tensor(
-                        out=stage[:].rearrange("p (n j) -> p n j", j=PACK),
-                        in0=piece[:, :, pa:pe].rearrange("p j n -> p n j"),
-                        in1=hi_bf[:, PACK * a : PACK * e].rearrange("p (n j) -> p n j", j=PACK),
-                        op=ALU.subtract,
-                    )
-            elif kind == "qhi":
-                a, e = step[1], step[2]
-                nc.vector.quantize_mx(out=hi_codes[:, a:e].bitcast(FP8X4), scales=hi_scales[:, a:e], in_=hi_bf[:, PACK * a : PACK * e])
-            elif kind == "qlo":
-                a, e = step[1], step[2]
-                src = lo_stage[a][:] if a in lo_stage else lo_bf[:, PACK * a : PACK * e]
-                nc.vector.quantize_mx(out=lo_codes[:, a:e].bitcast(FP8X4), scales=lo_scales[:, a:e], in_=src)
-            elif kind == "xc":
-                a, e = step[1], step[2]
-                piece, pa, pe = raw_view("x", a, e)
-                tag = "gpsimd_stage" if step[3] == "G" else "x_bf_%d" % a
-                stage = keep.tile([P, PACK * (e - a)], BF16, name=tag, align_bytes=256)
-                copy_on(step[3], stage[:], piece[:, :, pa:pe])
-                x_bf[a] = stage
-            elif kind == "qx":
-                a, e = step[1], step[2]
-                nc.vector.quantize_mx(out=x_codes[:, a:e].bitcast(FP8X4), scales=x_scales[:, a:e], in_=x_bf[a][:])
-            elif kind == "mm":
-                t, c = step[1], step[2]
-                bank = psum.tile([P, BANK], F32, name="bank")
-                t_cols = slice(t * P, (t + 1) * P)
-                n_cols = slice(c * BANK, (c + 1) * BANK)
-                for codes, scales, first in ((hi_codes, hi_scales, True), (lo_codes, lo_scales, False)):
+        def copy_bias(chunk):
+            nc.scalar.copy(
+                out=bias_rows[:, chunk * CHUNK : (chunk + 1) * CHUNK].rearrange("q (p c) -> q p c", c=PACK),
+                in_=bias_banks[chunk][:].rearrange("q (c p) -> q p c", c=PACK),
+            )
+
+        def multiply_ready(emptied):
+            while len(sums) < min(len(order), emptied + PSUM_BANKS):
+                tile, chunk = order[len(sums)]
+                t_cols = slice(tile * P, (tile + 1) * P)
+                n_cols = slice(chunk * CHUNK, (chunk + 1) * CHUNK)
+                if quantised["x"] < t_cols.stop or min(quantised["hi"], quantised["lo"]) < n_cols.stop:
+                    break
+                bank = psum.tile([P, CHUNK], F32, name="bank")
+                for part in ("hi", "lo"):
+                    codes, scales = mx[part]
                     nc.tensor.matmul_mx(
                         out=bank[:],
                         lhsT=x_codes[:, t_cols].bitcast(FP8X4),
                         lhsT_scale=x_scales[:, t_cols],
                         rhs=codes[:, n_cols].bitcast(FP8X4),
                         rhs_scale=scales[:, n_cols],
-                        start=first,
-                        stop=not first,
+                        start=part == "hi",
+                        stop=part == "lo",
                     )
-                banks[(t, c)] = bank
-            elif kind == "add":
-                t, a, e = step[1], step[2], step[3]
-                if t not in res:
-                    res[t] = keep.tile([P, N], F32, name="res_%d" % t, align_bytes=256)
-                c = a // BANK
-                nc.vector.tensor_tensor(
-                    out=res[t][:, a:e], in0=banks[(t, c)][:, a - c * BANK : e - c * BANK], in1=bias_rows[:, a:e], op=ALU.add
-                )
-            elif kind == "gelu":
-                t, a, e = step[1], step[2], step[3]
-                nc.scalar.activation(out=res[t][:, a:e], in_=res[t][:, a:e], func=GELU)
-            else:
-                t, a, e = step[1], step[2], step[3]
-                nc.sync.dma_start(out=out[t * P : (t + 1) * P, a:e], in_=res[t][:, a:e])
+                sums.append(bank)
+
+        def finish(position):
+            tile, chunk = order[position]
+            n_cols = slice(chunk * CHUNK, (chunk + 1) * CHUNK)
+            if tile not in results:
+                results[tile] = keep.tile([P, N], F32, name="result_%d" % tile, align_bytes=ALIGN)
+            block = results[tile][:, n_cols]
+            nc.vector.tensor_tensor(out=block, in0=sums[position][:], in1=bias_rows[:, n_cols], op=ALU.add)
+            nc.scalar.activation(out=block, in_=block, func=GELU)
+            nc.sync.dma_start(out=out[tile * P : (tile + 1) * P, n_cols], in_=block)
+
+        ctx.enter_context(tc.manual_schedule())
+
+        nc.scalar.dma_start(out=bias_cols[:], in_=b.rearrange("(g p c) -> p g c", p=P, c=PACK))
+        nc.gpsimd.memset(warm_in[:], 0.0)
+        nc.scalar.activation(out=warm_out[:], in_=warm_in[:], func=GELU)
+        make_identity(nc, identity[:])
+
+        for name, first, end in LOADS:
+            piece = keep.tile([P, PACK, end - first], F32, name="raw_%s_%d" % (name, first), align_bytes=ALIGN)
+            source = {"w": w, "x": x}[name]
+            nc.sync.dma_start(out=piece[:], in_=source[:, first:end].rearrange("(p j) n -> p j n", j=PACK))
+            loaded[name].append((first, end, piece))
+        for chunk in range(CHUNKS):
+            spread_bias(chunk)
+
+        upper_halves(nc.vector.tensor_copy, 128, 256)
+        for first, end in ((0, 128), (256, 384), (384, 512)):
+            upper_halves(nc.scalar.copy, first, end)
+        copy_bias(0)
+        upper_halves(nc.scalar.copy, 512, 768)
+        upper_halves(nc.scalar.copy, 768, 1024)
+        cast_x_on_scalar(0, 256)
+        cast_x_on_scalar(256, 512)
+        upper_halves(nc.scalar.copy, 1024, 1280)
+        copy_bias(1)
+        copy_bias(2)
+        cast_x_on_scalar(512, 640)
+        cast_x_on_scalar(640, 896)
+        upper_halves(nc.scalar.copy, 1280, 1536)
+        cast_x_on_scalar(896, 1024)
+
+        mask_hi(128, 256)
+        mask_hi(0, 128)
+        low_on_vector(128, 256)
+        low_on_vector(0, 128)
+        mask_hi(256, 512)
+        quantize("hi", 0, 256)
+        low_on_vector(256, 384)
+        low_on_vector(384, 512)
+        mask_hi(512, 768)
+        quantize("lo", 0, 512)
+        quantize("hi", 256, 512)
+        low_on_vector(512, 768)
+        mask_hi(768, 1024)
+        quantize("x", 0, 256)
+        low_on_vector(768, 1024)
+        quantize("hi", 512, 1024)
+        quantize("lo", 512, 1024)
+        mask_hi(1024, 1152)
+        low_on_gpsimd(1024, 1152)
+        quantize("x", 256, 512)
+
+        after = {
+            2: [(mask_hi, 1152, 1280), (quantize, "lo", 1024, 1152), (low_on_gpsimd, 1152, 1280), (quantize, "x", 512, 640)],
+            5: [(mask_hi, 1280, 1536), (quantize, "lo", 1152, 1280), (low_on_gpsimd, 1280, 1408), (quantize, "x", 640, 896)],
+            8: [(quantize, "x", 896, 1024), (quantize, "lo", 1280, 1408), (low_on_gpsimd, 1408, 1536), (quantize, "hi", 1024, 1536)],
+            11: [(quantize, "lo", 1408, 1536), (cast_x_on_gpsimd, 1024, 1280)],
+            16: [(quantize, "x", 1024, 1280), (cast_x_on_gpsimd, 1280, 1536)],
+            26: [(quantize, "x", 1280, 1536)],
+        }
+        for position in range(len(order)):
+            multiply_ready(position)
+            finish(position)
+            for step in after.get(position, []):
+                step[0](*step[1:])

from contextlib import ExitStack

import concourse.mybir as mybir
from concourse.masks import make_identity

K, N, T = 512, 1536, 1536
FLOPS = 2 * 2 * K * N * T

F32 = mybir.dt.float32
BF16 = mybir.dt.bfloat16
I32 = mybir.dt.int32
U32 = mybir.dt.uint32
U8 = mybir.dt.uint8
FP8X4 = mybir.dt.float8_e4m3fn_x4
ALU = mybir.AluOpType
GELU = mybir.ActivationFunctionType.Gelu_apprx_tanh

P = 128
PACK = 4
CHUNK = 512
PSUM_BANKS = 8
ALIGN = 256
CHUNKS = N // CHUNK
ROW_TILES = T // P
HI_MASK = -983056
EARLY_TILES = 8

LOADS = (
    ("w", 0, 256), ("w", 256, 384), ("w", 384, 512), ("w", 512, 768), ("w", 768, 1024),
    ("x", 0, 256), ("x", 256, 512), ("w", 1024, 1280), ("x", 512, 1024), ("w", 1280, 1536),
    ("x", 1024, 1536),
)


def bank_order():
    order = [(tile, chunk) for chunk in range(2) for tile in range(2)]
    order += [(tile, chunk) for tile in range(2, EARLY_TILES) for chunk in range(2)]
    order += [(tile, CHUNKS - 1) for tile in range(EARLY_TILES)]
    order += [(tile, chunk) for tile in range(EARLY_TILES, ROW_TILES) for chunk in range(CHUNKS)]
    return order


def tile_mix_hilo_tm_gelu_kernel(tc, w, x, b, out):
    nc = tc.nc

    with ExitStack() as ctx:
        keep = ctx.enter_context(tc.tile_pool(name="keep", bufs=1))
        psum = ctx.enter_context(tc.psum_pool(name="psum", bufs=PSUM_BANKS))

        hi_bf = keep.tile([P, PACK * N], BF16, align_bytes=ALIGN)
        lo_bf = keep.tile([P, PACK * (N - CHUNK)], BF16, align_bytes=ALIGN)
        hi_codes = keep.tile([P, N], U32, align_bytes=ALIGN)
        lo_codes = keep.tile([P, N], U32, align_bytes=ALIGN)
        x_codes = keep.tile([P, T], U32, align_bytes=ALIGN)
        hi_scales = keep.tile([P, N], U8, align_bytes=ALIGN)
        lo_scales = keep.tile([P, N], U8, align_bytes=ALIGN)
        x_scales = keep.tile([P, T], U8, align_bytes=ALIGN)
        bias_cols = keep.tile([P, CHUNKS, PACK], F32)
        bias_rows = keep.tile([P, N], F32, align_bytes=ALIGN)
        identity = keep.tile([P, P], F32)
        warm_in = keep.tile([P, 8], F32)
        warm_out = keep.tile([P, 8], F32)

        mx = {"hi": (hi_codes, hi_scales), "lo": (lo_codes, lo_scales), "x": (x_codes, x_scales)}
        loaded = {"w": [], "x": []}
        staged = {}
        quantised = {"hi": 0, "lo": 0, "x": 0}
        bias_banks = []
        sums = []
        results = {}
        order = bank_order()

        def raw(name, first, end):
            for piece_first, piece_end, piece in loaded[name]:
                if piece_first <= first and end <= piece_end:
                    return piece, slice(first - piece_first, end - piece_first)
            raise ValueError(name)

        def packed(tile, first, end):
            return tile[:, PACK * first : PACK * end]

        def by_rows(rows, run):
            return rows.rearrange("p j (c i) -> p c j i", i=run)

        def by_words(words, run):
            return words.rearrange("p (c i j) -> p c j i", i=run, j=PACK)

        def gpsimd_stage(operand, first, end):
            stage = keep.tile([P, PACK * (end - first)], BF16, name="gpsimd_stage", align_bytes=ALIGN)
            staged[(operand, first)] = stage
            return stage[:].rearrange("p (n j) -> p n j", j=PACK)

        def upper_halves(copy, first, end):
            piece, cols = raw("w", first, end)
            halves = piece[:].bitcast(BF16).rearrange("p j (n h) -> p j n h", h=2)
            copy(out=by_words(packed(hi_bf, first, end), 4), in_=by_rows(halves[:, :, cols, 1], 4))

        def mask_hi(first, end):
            pairs = packed(hi_bf, first, end).bitcast(I32)
            nc.vector.tensor_scalar(out=pairs, in0=pairs, scalar1=HI_MASK, scalar2=None, op0=ALU.bitwise_and)

        def low_on_vector(first, end):
            piece, cols = raw("w", first, end)
            nc.vector.tensor_tensor(
                out=by_words(packed(lo_bf, first, end), 2),
                in0=by_rows(piece[:, :, cols], 2),
                in1=by_words(packed(hi_bf, first, end), 2),
                op=ALU.subtract,
            )

        def low_on_gpsimd(first, end):
            piece, cols = raw("w", first, end)
            nc.gpsimd.tensor_tensor(
                out=gpsimd_stage("lo", first, end),
                in0=piece[:, :, cols].rearrange("p j n -> p n j"),
                in1=packed(hi_bf, first, end).rearrange("p (n j) -> p n j", j=PACK),
                op=ALU.subtract,
            )

        def cast_x_on_scalar(first, end):
            piece, cols = raw("x", first, end)
            stage = keep.tile([P, PACK * (end - first)], BF16, name="x_bf_%d" % first, align_bytes=ALIGN)
            staged[("x", first)] = stage
            nc.scalar.copy(out=by_words(stage[:], 4), in_=by_rows(piece[:, :, cols], 4))

        def cast_x_on_gpsimd(first, end):
            piece, cols = raw("x", first, end)
            nc.gpsimd.tensor_scalar(
                out=gpsimd_stage("x", first, end),
                in0=piece[:, :, cols].rearrange("p j n -> p n j"),
                scalar1=1.0,
                scalar2=0.0,
                op0=ALU.mult,
                op1=ALU.add,
            )

        def quantize(operand, first, end):
            if (operand, first) in staged:
                values = staged[(operand, first)][:]
            else:
                values = packed({"hi": hi_bf, "lo": lo_bf}[operand], first, end)
            codes, scales = mx[operand]
            nc.vector.quantize_mx(out=codes[:, first:end].bitcast(FP8X4), scales=scales[:, first:end], in_=values)
            quantised[operand] = end

        def spread_bias(chunk):
            bank = psum.tile([P, CHUNK], F32, name="bank")
            for c in range(PACK):
                column = bias_cols[:, chunk, c : c + 1].to_broadcast([P, P])
                nc.tensor.transpose(bank[:, c * P : (c + 1) * P], column, identity[:])
            bias_banks.append(bank)

        def copy_bias(chunk):
            nc.scalar.copy(
                out=bias_rows[:, chunk * CHUNK : (chunk + 1) * CHUNK].rearrange("q (p c) -> q p c", c=PACK),
                in_=bias_banks[chunk][:].rearrange("q (c p) -> q p c", c=PACK),
            )

        def multiply_ready(emptied):
            while len(sums) < min(len(order), emptied + PSUM_BANKS):
                tile, chunk = order[len(sums)]
                t_cols = slice(tile * P, (tile + 1) * P)
                n_cols = slice(chunk * CHUNK, (chunk + 1) * CHUNK)
                if quantised["x"] < t_cols.stop or min(quantised["hi"], quantised["lo"]) < n_cols.stop:
                    break
                bank = psum.tile([P, CHUNK], F32, name="bank")
                for part in ("hi", "lo"):
                    codes, scales = mx[part]
                    nc.tensor.matmul_mx(
                        out=bank[:],
                        lhsT=x_codes[:, t_cols].bitcast(FP8X4),
                        lhsT_scale=x_scales[:, t_cols],
                        rhs=codes[:, n_cols].bitcast(FP8X4),
                        rhs_scale=scales[:, n_cols],
                        start=part == "hi",
                        stop=part == "lo",
                    )
                sums.append(bank)

        def finish(position):
            tile, chunk = order[position]
            n_cols = slice(chunk * CHUNK, (chunk + 1) * CHUNK)
            if tile not in results:
                results[tile] = keep.tile([P, N], F32, name="result_%d" % tile, align_bytes=ALIGN)
            block = results[tile][:, n_cols]
            nc.vector.tensor_tensor(out=block, in0=sums[position][:], in1=bias_rows[:, n_cols], op=ALU.add)
            nc.scalar.activation(out=block, in_=block, func=GELU)
            nc.sync.dma_start(out=out[tile * P : (tile + 1) * P, n_cols], in_=block)

        ctx.enter_context(tc.manual_schedule())

        nc.scalar.dma_start(out=bias_cols[:], in_=b.rearrange("(g p c) -> p g c", p=P, c=PACK))
        nc.gpsimd.memset(warm_in[:], 0.0)
        nc.scalar.activation(out=warm_out[:], in_=warm_in[:], func=GELU)
        make_identity(nc, identity[:])

        for name, first, end in LOADS:
            piece = keep.tile([P, PACK, end - first], F32, name="raw_%s_%d" % (name, first), align_bytes=ALIGN)
            source = {"w": w, "x": x}[name]
            nc.sync.dma_start(out=piece[:], in_=source[:, first:end].rearrange("(p j) n -> p j n", j=PACK))
            loaded[name].append((first, end, piece))
        for chunk in range(CHUNKS):
            spread_bias(chunk)

        upper_halves(nc.vector.tensor_copy, 128, 256)
        for first, end in ((0, 128), (256, 384), (384, 512)):
            upper_halves(nc.scalar.copy, first, end)
        copy_bias(0)
        upper_halves(nc.scalar.copy, 512, 768)
        upper_halves(nc.scalar.copy, 768, 1024)
        cast_x_on_scalar(0, 256)
        cast_x_on_scalar(256, 512)
        upper_halves(nc.scalar.copy, 1024, 1280)
        copy_bias(1)
        copy_bias(2)
        cast_x_on_scalar(512, 640)
        cast_x_on_scalar(640, 896)
        upper_halves(nc.scalar.copy, 1280, 1536)
        cast_x_on_scalar(896, 1024)

        mask_hi(128, 256)
        mask_hi(0, 128)
        low_on_vector(128, 256)
        low_on_vector(0, 128)
        mask_hi(256, 512)
        quantize("hi", 0, 256)
        low_on_vector(256, 384)
        low_on_vector(384, 512)
        mask_hi(512, 768)
        quantize("lo", 0, 512)
        quantize("hi", 256, 512)
        low_on_vector(512, 768)
        mask_hi(768, 1024)
        quantize("x", 0, 256)
        low_on_vector(768, 1024)
        quantize("hi", 512, 1024)
        quantize("lo", 512, 1024)
        mask_hi(1024, 1152)
        low_on_gpsimd(1024, 1152)
        quantize("x", 256, 512)

        after = {
            2: [(mask_hi, 1152, 1280), (quantize, "lo", 1024, 1152), (low_on_gpsimd, 1152, 1280), (quantize, "x", 512, 640)],
            5: [(mask_hi, 1280, 1536), (quantize, "lo", 1152, 1280), (low_on_gpsimd, 1280, 1408), (quantize, "x", 640, 896)],
            8: [(quantize, "x", 896, 1024), (quantize, "lo", 1280, 1408), (low_on_gpsimd, 1408, 1536), (quantize, "hi", 1024, 1536)],
            11: [(quantize, "lo", 1408, 1536), (cast_x_on_gpsimd, 1024, 1280)],
            16: [(quantize, "x", 1024, 1280), (cast_x_on_gpsimd, 1280, 1536)],
            26: [(quantize, "x", 1280, 1536)],
        }
        for position in range(len(order)):
            multiply_ready(position)
            finish(position)
            for step in after.get(position, []):
                step[0](*step[1:])
